import numpy as np
import ml_dtypes


def mxq(x, axis, fmt="e4m3"):
    dtype, down = {"e4m3": (ml_dtypes.float8_e4m3fn, 7), "e5m2": (ml_dtypes.float8_e5m2, 14)}[fmt]
    v = np.moveaxis(np.asarray(x, np.float32).astype(ml_dtypes.bfloat16).astype(np.float64), axis, -1)
    blocks = v.reshape(v.shape[:-1] + (-1, 32))
    amax = np.abs(blocks).max(-1, keepdims=True)
    byte = np.maximum(np.where(amax > 0, np.frexp(amax)[1] - 1 + 127, 0) - down, 1)
    scale = np.exp2(byte - 127.0)
    codes = (blocks / scale).astype(np.float32).astype(dtype).astype(np.float64)
    return np.moveaxis((codes * scale).reshape(v.shape), -1, axis)


WIDE = False


def mx_kscale(k):
    if not WIDE:
        return np.ones(k)
    levels = np.array([10, -10, 5, -5, 0])
    if k % 512:
        return np.exp2(np.random.permutation(np.resize(levels, k // 32))).repeat(32)
    a = np.empty((k // 512, 16))
    for p in range(k // 512):
        a[p, :8] = np.random.permutation(np.resize(levels, 8))
        for g in range(8):
            far = levels[np.abs(levels - a[p, g]) >= 10]
            a[p, g + 8] = far[np.random.randint(len(far))]
    return np.exp2(a.ravel()).repeat(32)


def f64(x):
    return np.asarray(x).astype(np.float64)


def striped(idx):
    return np.tile(idx.reshape(-1, 16).T, (8, 1)).astype(np.uint16)


def unstriped(offs):
    return offs[:16].T.reshape(-1).astype(np.int64)


def striped8(idx):
    return np.concatenate([v.reshape(-1, 16).T for v in idx]).astype(np.uint16)


def unstriped8(offs):
    return np.stack([offs[16 * g:16 * g + 16].T.reshape(-1) for g in range(8)]).astype(np.int64)


E2M1 = np.array([0.0, 0.5, 1.0, 1.5, 2.0, 3.0, 4.0, 6.0, -0.0, -0.5, -1.0, -1.5, -2.0, -3.0, -4.0, -6.0])


def pack_weight(w, fmt):
    k, n = w.shape
    w = f64(np.asarray(w, np.float32).astype(ml_dtypes.bfloat16)).reshape(k // 32, 32, n)
    amax = np.abs(w).max(1)
    if fmt == "e4m3":
        byte = np.frexp(amax)[1] - 1 + 127 - 7
    else:
        mant, ex = np.frexp(amax / 6.0)
        byte = np.where(mant > 0.5, ex, ex - 1) + 127
    byte = np.clip(np.where(amax > 0, byte, 1), 1, 254)
    scaled = (w * np.exp2(127.0 - byte)[:, None, :]).reshape(k, n).astype(np.float32)
    by_word = np.ascontiguousarray(scaled.reshape(k // 512, 128, 4, n).transpose(0, 1, 3, 2))
    if fmt == "e4m3":
        words = by_word.astype(ml_dtypes.float8_e4m3fn).view(np.uint8)
    else:
        c = by_word.astype(ml_dtypes.float4_e2m1fn).view(np.uint8) & 0xF
        words = (c[..., 0::2] | (c[..., 1::2] << 4)).reshape(k // 512, 128, 2 * n)
    return np.ascontiguousarray(words), np.ascontiguousarray(byte.astype(np.uint8).reshape(k // 512, 16, n))


def unpack_weight(words, scales, fmt):
    g, _, n = scales.shape
    words = np.ascontiguousarray(words).reshape(g, 128, n, -1)
    if fmt == "e4m3":
        vals = words.view(ml_dtypes.float8_e4m3fn).astype(np.float64)
    else:
        nib = np.empty((g, 128, n, 4), np.uint8)
        nib[..., 0::2] = words & 0xF
        nib[..., 1::2] = words >> 4
        vals = E2M1[nib]
    vals = vals * np.repeat(np.exp2(scales.astype(np.float64) - 127.0), 8, axis=1)[..., None]
    return vals.transpose(0, 1, 3, 2).reshape(g * 512, n)


def pack_table(v):
    words, scales = pack_weight(v, "e4m3")
    return np.concatenate([words.reshape(words.shape[0], -1), scales.reshape(scales.shape[0], -1)], axis=1)


def unpack_table(tab):
    g, t = tab.shape[0], tab.shape[1] // 528
    return unpack_weight(tab[:, :512 * t].reshape(g, 128, t, 4), tab[:, 512 * t:].reshape(g, 16, t), "e4m3")


def gelu(v):
    return 0.5 * v * (1.0 + np.tanh(np.sqrt(2.0 / np.pi) * (v + 0.044715 * v**3)))


K, M, T, S = 512, 256, 1024, 512


def setup_inputs():
    n = np.random.standard_normal
    s = mx_kscale(K)[:, None]
    s2 = mx_kscale(512)[:, None]
    p_w4 = pack_weight(n((K, M)) / np.sqrt(K) / s, "e2m1")
    return {
        "tab": pack_table(n((K, T)) * s),
        "w4_words": p_w4[0],
        "w4_scales": p_w4[1],
        "c": (n((512, S)) * s2).astype(np.float32),
        "u": (n((512, M)) / np.sqrt(512) / s2).astype(np.float32),
        "b": (0.3 * n(256)).astype(np.float32),
        "wgo": np.repeat(np.random.uniform(0.5, 2.0, (8, S)), 16, axis=0).astype(np.float32),
        "offs": striped(np.random.permutation(T)[:S]),
        "offs2": striped8(np.stack([np.random.permutation(T)[:S] for _ in range(8)])),
    }


def reference(tab, w4_words, w4_scales, c, u, b, wgo, offs, offs2):
    tab_ = unpack_table(tab)[:, unstriped(offs)]
    w4_ = unpack_weight(w4_words, w4_scales, "e2m1")
    c_ = mxq(f64(c), 0, "e4m3")
    u_ = mxq(f64(u), 0, "e4m3")
    y = w4_.T @ tab_ + u_.T @ c_
    place = unstriped8(offs2)[np.arange(M) % 128 // 16]
    out = np.zeros((M, T))
    out[np.arange(M)[:, None], place] = f64(wgo)[np.arange(M) % 128] * (gelu(y + f64(b)[:, None]))
    return out

@@ -1,0 +1,150 @@
+from contextlib import ExitStack
+
+import concourse.mybir as mybir
+
+K, M, T, S = 512, 256, 1024, 512
+FLOPS = 2 * 2 * K * M * S
+
+F32 = mybir.dt.float32
+BF16 = mybir.dt.bfloat16
+I32 = mybir.dt.int32
+U32 = mybir.dt.uint32
+U16 = mybir.dt.uint16
+U8 = mybir.dt.uint8
+FP8X4 = mybir.dt.float8_e4m3fn_x4
+FP4X4 = mybir.dt.float4_e2m1fn_x4
+GELU = mybir.ActivationFunctionType.Gelu_apprx_tanh
+MULT = mybir.AluOpType.mult
+
+P = 128
+PACK = 4
+LANES = 16
+HALF = S // 2
+CHUNKS = ((0, 128), (128, 128), (256, 256))
+
+
+def interleave(copy, grouped, raw):
+    copy(
+        grouped.rearrange("p (c i) t -> p c t i", i=PACK),
+        raw.rearrange("p t (c i) -> p c t i", i=PACK),
+    )
+
+
+def tile_list_tabhs_d_gelu_kernel(tc, tab, w4_words, w4_scales, c, u, b, wgo, offs, offs2, out):
+    nc = tc.nc
+    with ExitStack() as ctx:
+        keep = ctx.enter_context(tc.tile_pool(name="keep", bufs=1))
+        psum = ctx.enter_context(tc.psum_pool(name="psum", bufs=1))
+
+        pick = keep.tile([P, S // LANES], U16, name="pick")
+        place = keep.tile([P, S // LANES], U16, name="place")
+        tab_words = keep.tile([P, T], I32, name="tab_words", align_bytes=64)
+        tab_plane = keep.tile([P, T], U8, name="tab_plane", align_bytes=64)
+        w4_codes = keep.tile([P, 2 * M], U8, name="w4_codes", align_bytes=64)
+        w4_plane = keep.tile([P, M], U8, name="w4_plane", align_bytes=64)
+        u_raw = keep.tile([P, PACK, M], F32, name="u_raw")
+        c_raw = [keep.tile([P, PACK, HALF], F32, name="c_raw%d" % h, tag="c_raw%d" % h) for h in range(2)]
+        weight = [keep.tile([P, HALF], F32, name="weight%d" % h) for h in range(2)]
+        bias = keep.tile([P, 2, 8], F32, name="bias")
+        pages = [keep.tile([P, T], F32, name="page%d" % m) for m in range(2)]
+        warm_in = keep.tile([P, 1], F32, name="warm_in")
+        warm_out = keep.tile([P, 1], F32, name="warm_out")
+
+        nc.vector.memset(tab_plane[:].bitcast(I32), 0)
+        nc.vector.memset(warm_in[:], 0.0)
+        nc.vector.memset(w4_plane[:].bitcast(I32), 0)
+        nc.scalar.activation(warm_out[:], warm_in[:], GELU)
+        for m in range(2):
+            nc.vector.memset(pages[m][:], 0.0)
+
+        nc.gpsimd.dma_start(w4_codes[:].bitcast(I32), w4_words[0].bitcast(I32))
+
+        c_rows = c.rearrange("(p t) j -> p t j", t=PACK)
+        tab_scales = tab[0, K * T :].rearrange("(q t) -> q t", t=T)
+        nc.sync.dma_start(pick[:], offs)
+        for q in range(4):
+            nc.sync.dma_start(tab_plane[32 * q : 32 * q + 4, :].bitcast(I32), tab_scales[4 * q : 4 * q + 4, :].bitcast(I32))
+        nc.sync.dma_start(u_raw[:], u.rearrange("(p t) n -> p t n", t=PACK))
+        nc.sync.dma_start(c_raw[0][:], c_rows[:, :, 0:HALF])
+        nc.sync.dma_start(tab_words[:], tab[0, 0 : K * T].rearrange("(p x) -> p x", p=P).bitcast(I32))
+        for q in range(4):
+            nc.sync.dma_start(w4_plane[32 * q : 32 * q + 4, :].bitcast(I32), w4_scales[0, 4 * q : 4 * q + 4, :].bitcast(I32))
+        nc.sync.dma_start(place[:], offs2)
+        with nc.allow_non_contiguous_dma(reason="one bias value a partition"):
+            nc.sync.dma_start(bias[:, :, 0], b.rearrange("(m p) -> p m", p=P))
+        nc.sync.dma_start(weight[0][:], wgo[:, 0:HALF])
+        nc.sync.dma_start(c_raw[1][:], c_rows[:, :, HALF:S])
+        nc.sync.dma_start(weight[1][:], wgo[:, HALF:S])
+
+        picked_plane = keep.tile([P, S], U8, name="picked_plane", align_bytes=64)
+        nc.vector.tensor_copy(picked_plane[:], tab_plane[:].indirect(pick[:]))
+
+        u_grouped = keep.tile([P, M, PACK], BF16, name="u_grouped", align_bytes=64)
+        u_codes = keep.tile([P, M], U32, name="u_codes", align_bytes=64)
+        u_plane = keep.tile([P, M], U8, name="u_plane", align_bytes=64)
+        interleave(nc.scalar.copy, u_grouped[:], u_raw[:])
+        nc.vector.quantize_mx(u_codes[:].bitcast(FP8X4), u_plane[:], u_grouped[:].rearrange("p n t -> p (n t)"))
+
+        c_codes = []
+        c_plane = []
+        picked_words = []
+
+        def quantise_c(i, copy):
+            j0, width = CHUNKS[i]
+            grouped = keep.tile([P, width, PACK], BF16, name="c_grouped%d" % i, align_bytes=64)
+            codes = keep.tile([P, width], U32, name="c_codes%d" % i, align_bytes=64)
+            plane = keep.tile([P, width], U8, name="c_plane%d" % i, align_bytes=64)
+            interleave(copy, grouped[:], c_raw[j0 // HALF][:, :, j0 % HALF : j0 % HALF + width])
+            nc.vector.quantize_mx(codes[:].bitcast(FP8X4), plane[:], grouped[:].rearrange("p n t -> p (n t)"))
+            c_codes.append(codes)
+            c_plane.append(plane)
+
+        def gather_words(i):
+            j0, width = CHUNKS[i]
+            words = keep.tile([P, width], U32, name="picked_words%d" % i, align_bytes=64)
+            nc.vector.tensor_copy(words[:], tab_words[:].bitcast(U32).indirect(pick[:, j0 // LANES : (j0 + width) // LANES]))
+            picked_words.append(words)
+
+        def project(i, m, tag):
+            j0, width = CHUNKS[i]
+            acc = psum.tile([P, width], F32, name="acc%d_%d" % (i, m))
+            rows = slice(m * P, (m + 1) * P)
+            pieces = width // P
+
+            def dense(start, stop):
+                nc.tensor.matmul_mx(acc[:], lhsT=u_codes[:, rows].bitcast(FP8X4), lhsT_scale=u_plane[:, rows],
+                                    rhs=c_codes[i][:].bitcast(FP8X4), rhs_scale=c_plane[i][:], start=start, stop=stop)
+
+            def looked_up(n, start, stop):
+                cols = slice(n * P, (n + 1) * P)
+                nc.tensor.matmul_mx(acc[:, cols], lhsT=w4_codes[:, 2 * m * P : 2 * (m + 1) * P].bitcast(FP4X4), lhsT_scale=w4_plane[:, rows],
+                                    rhs=picked_words[i][:, cols].bitcast(FP8X4), rhs_scale=picked_plane[:, j0 + n * P : j0 + (n + 1) * P],
+                                    start=start, stop=stop)
+
+            if j0 < HALF:
+                dense(True, False)
+                for n in range(pieces):
+                    looked_up(n, False, n == pieces - 1)
+            else:
+                for n in range(pieces):
+                    looked_up(n, n == 0, False)
+                dense(False, True)
+
+            act = keep.tile([P, width], F32, name="act%d_%d" % (i, m), tag=tag)
+            nc.scalar.activation(act[:], acc[:], GELU, bias=bias[:, m, 0:1])
+            nc.vector.tensor_tensor(pages[m][:].indirect(place[:, j0 // LANES : (j0 + width) // LANES]), act[:],
+                                    weight[j0 // HALF][:, j0 % HALF : j0 % HALF + width], MULT)
+
+        quantise_c(0, nc.vector.tensor_copy)
+        quantise_c(1, nc.scalar.copy)
+        for i in range(3):
+            gather_words(i)
+        project(0, 0, "act00")
+        project(0, 1, "act01")
+        project(1, 0, "act10")
+        quantise_c(2, nc.scalar.copy)
+        project(1, 1, "c_raw1")
+        project(2, 0, "act20")
+        project(2, 1, "act21")
+        for m in range(2):
+            nc.sync.dma_start(out[m * P : (m + 1) * P, :], pages[m][:])

@@ -39,7 +39,7 @@ def tile_list_tabhs_d_gelu_kernel(tc, tab, w4_words, w4_scales, c, u, b, wgo, of
         pick = keep.tile([P, S // LANES], U16, name="pick")
         place = keep.tile([P, S // LANES], U16, name="place")
         tab_words = keep.tile([P, T], I32, name="tab_words", align_bytes=64)
-        tab_plane = keep.tile([P, T], U8, name="tab_plane", align_bytes=64)
+        tab_plane = keep.tile([P, T], U8, name="tab_plane", tag="tab_plane", align_bytes=64)
         w4_codes = keep.tile([P, 2 * M], U8, name="w4_codes", align_bytes=64)
         w4_plane = keep.tile([P, M], U8, name="w4_plane", align_bytes=64)
         u_raw = keep.tile([P, PACK, M], F32, name="u_raw")
@@ -57,21 +57,25 @@ def tile_list_tabhs_d_gelu_kernel(tc, tab, w4_words, w4_scales, c, u, b, wgo, of
         for m in range(2):
             nc.vector.memset(pages[m][:], 0.0)
 
-        nc.gpsimd.dma_start(w4_codes[:].bitcast(I32), w4_words[0].bitcast(I32))
-
         c_rows = c.rearrange("(p t) j -> p t j", t=PACK)
         tab_scales = tab[0, K * T :].rearrange("(q t) -> q t", t=T)
+
+        def load_scale_rows(queue, plane, rows, q):
+            queue.dma_start(plane[32 * q : 32 * q + 4, :].bitcast(I32), rows[4 * q : 4 * q + 4, :].bitcast(I32))
+
+        nc.gpsimd.dma_start(w4_codes[:].bitcast(I32), w4_words[0].bitcast(I32))
+        with nc.allow_non_contiguous_dma(reason="one bias value a partition"):
+            nc.gpsimd.dma_start(bias[:, :, 0], b.rearrange("(m p) -> p m", p=P))
+
+        nc.sync.dma_start(u_raw[:], u.rearrange("(p t) n -> p t n", t=PACK))
         nc.sync.dma_start(pick[:], offs)
         for q in range(4):
-            nc.sync.dma_start(tab_plane[32 * q : 32 * q + 4, :].bitcast(I32), tab_scales[4 * q : 4 * q + 4, :].bitcast(I32))
-        nc.sync.dma_start(u_raw[:], u.rearrange("(p t) n -> p t n", t=PACK))
+            load_scale_rows(nc.sync, tab_plane, tab_scales, q)
         nc.sync.dma_start(c_raw[0][:], c_rows[:, :, 0:HALF])
         nc.sync.dma_start(tab_words[:], tab[0, 0 : K * T].rearrange("(p x) -> p x", p=P).bitcast(I32))
         for q in range(4):
-            nc.sync.dma_start(w4_plane[32 * q : 32 * q + 4, :].bitcast(I32), w4_scales[0, 4 * q : 4 * q + 4, :].bitcast(I32))
+            load_scale_rows(nc.sync, w4_plane, w4_scales[0], q)
         nc.sync.dma_start(place[:], offs2)
-        with nc.allow_non_contiguous_dma(reason="one bias value a partition"):
-            nc.sync.dma_start(bias[:, :, 0], b.rearrange("(m p) -> p m", p=P))
         nc.sync.dma_start(weight[0][:], wgo[:, 0:HALF])
         nc.sync.dma_start(c_raw[1][:], c_rows[:, :, HALF:S])
         nc.sync.dma_start(weight[1][:], wgo[:, HALF:S])
@@ -80,7 +84,7 @@ def tile_list_tabhs_d_gelu_kernel(tc, tab, w4_words, w4_scales, c, u, b, wgo, of
         nc.vector.tensor_copy(picked_plane[:], tab_plane[:].indirect(pick[:]))
 
         u_grouped = keep.tile([P, M, PACK], BF16, name="u_grouped", align_bytes=64)
-        u_codes = keep.tile([P, M], U32, name="u_codes", align_bytes=64)
+        u_codes = keep.tile([P, M], U32, name="u_codes", tag="tab_plane", align_bytes=64)
         u_plane = keep.tile([P, M], U8, name="u_plane", align_bytes=64)
         interleave(nc.scalar.copy, u_grouped[:], u_raw[:])
         nc.vector.quantize_mx(u_codes[:].bitcast(FP8X4), u_plane[:], u_grouped[:].rearrange("p n t -> p (n t)"))
@@ -105,7 +109,7 @@ def tile_list_tabhs_d_gelu_kernel(tc, tab, w4_words, w4_scales, c, u, b, wgo, of
             nc.vector.tensor_copy(words[:], tab_words[:].bitcast(U32).indirect(pick[:, j0 // LANES : (j0 + width) // LANES]))
             picked_words.append(words)
 
-        def project(i, m, tag):
+        def project(i, m, act):
             j0, width = CHUNKS[i]
             acc = psum.tile([P, width], F32, name="acc%d_%d" % (i, m))
             rows = slice(m * P, (m + 1) * P)
@@ -130,21 +134,24 @@ def tile_list_tabhs_d_gelu_kernel(tc, tab, w4_words, w4_scales, c, u, b, wgo, of
                     looked_up(n, n == 0, False)
                 dense(False, True)
 
-            act = keep.tile([P, width], F32, name="act%d_%d" % (i, m), tag=tag)
-            nc.scalar.activation(act[:], acc[:], GELU, bias=bias[:, m, 0:1])
-            nc.vector.tensor_tensor(pages[m][:].indirect(place[:, j0 // LANES : (j0 + width) // LANES]), act[:],
+            nc.scalar.activation(act, acc[:], GELU, bias=bias[:, m, 0:1])
+            nc.vector.tensor_tensor(pages[m][:].indirect(place[:, j0 // LANES : (j0 + width) // LANES]), act,
                                     weight[j0 // HALF][:, j0 % HALF : j0 % HALF + width], MULT)
 
-        quantise_c(0, nc.vector.tensor_copy)
+        quantise_c(0, nc.scalar.copy)
+        gather_words(0)
         quantise_c(1, nc.scalar.copy)
-        for i in range(3):
-            gather_words(i)
-        project(0, 0, "act00")
-        project(0, 1, "act01")
-        project(1, 0, "act10")
+        gather_words(1)
+        gather_words(2)
+        act0 = keep.tile([P, 2, 128], F32, name="act0")
+        for m in range(2):
+            project(0, m, act0[:, m, :])
         quantise_c(2, nc.scalar.copy)
-        project(1, 1, "c_raw1")
-        project(2, 0, "act20")
-        project(2, 1, "act21")
+        act1 = keep.tile([P, 2, 128], F32, name="act1", tag="c_raw1")
+        for m in range(2):
+            project(1, m, act1[:, m, :])
+        act2 = keep.tile([P, 2, 256], F32, name="act2")
+        for m in range(2):
+            project(2, m, act2[:, m, :])
         for m in range(2):
             nc.sync.dma_start(out[m * P : (m + 1) * P, :], pages[m][:])

@@ -18,16 +18,38 @@ MULT = mybir.AluOpType.mult
 
 P = 128
 PACK = 4
-LANES = 16
+QUADRANT = 32
+GROUP = 16
+PAGES = M // P
 HALF = S // 2
+FP4_N = 128
+BIAS_PITCH = 8
+MX_ALIGN = 64
+
 CHUNKS = ((0, 128), (128, 128), (256, 256))
 
 
-def interleave(copy, grouped, raw):
-    copy(
+def round_and_interleave(nc, grouped, raw):
+    nc.scalar.copy(
         grouped.rearrange("p (c i) t -> p c t i", i=PACK),
         raw.rearrange("p t (c i) -> p c t i", i=PACK),
     )
+
+
+def quantise(nc, codes, plane, grouped):
+    nc.vector.quantize_mx(codes[:].bitcast(FP8X4), plane[:], grouped[:].rearrange("p x t -> p (x t)"))
+
+
+def load_scale_rows(nc, plane, rows):
+    for quad in range(P // QUADRANT):
+        nc.sync.dma_start(
+            plane[QUADRANT * quad : QUADRANT * quad + PACK, :].bitcast(I32),
+            rows[PACK * quad : PACK * (quad + 1), :].bitcast(I32),
+        )
+
+
+def list_columns(first, count):
+    return slice(first // GROUP, (first + count) // GROUP)
 
 
 def tile_list_tabhs_d_gelu_kernel(tc, tab, w4_words, w4_scales, c, u, b, wgo, offs, offs2, out):
@@ -36,17 +58,17 @@ def tile_list_tabhs_d_gelu_kernel(tc, tab, w4_words, w4_scales, c, u, b, wgo, of
         keep = ctx.enter_context(tc.tile_pool(name="keep", bufs=1))
         psum = ctx.enter_context(tc.psum_pool(name="psum", bufs=1))
 
-        pick = keep.tile([P, S // LANES], U16, name="pick")
-        place = keep.tile([P, S // LANES], U16, name="place")
-        tab_words = keep.tile([P, T], I32, name="tab_words", align_bytes=64)
-        tab_plane = keep.tile([P, T], U8, name="tab_plane", tag="tab_plane", align_bytes=64)
-        w4_codes = keep.tile([P, 2 * M], U8, name="w4_codes", align_bytes=64)
-        w4_plane = keep.tile([P, M], U8, name="w4_plane", align_bytes=64)
+        pick = keep.tile([P, S // GROUP], U16, name="pick")
+        place = keep.tile([P, S // GROUP], U16, name="place")
+        tab_words = keep.tile([P, T], I32, name="tab_words", align_bytes=MX_ALIGN)
+        tab_plane = keep.tile([P, T], U8, name="tab_plane", tag="tab_plane", align_bytes=MX_ALIGN)
+        w4_codes = keep.tile([P, 2 * M], U8, name="w4_codes", align_bytes=MX_ALIGN)
+        w4_plane = keep.tile([P, M], U8, name="w4_plane", align_bytes=MX_ALIGN)
         u_raw = keep.tile([P, PACK, M], F32, name="u_raw")
         c_raw = [keep.tile([P, PACK, HALF], F32, name="c_raw%d" % h, tag="c_raw%d" % h) for h in range(2)]
         weight = [keep.tile([P, HALF], F32, name="weight%d" % h) for h in range(2)]
-        bias = keep.tile([P, 2, 8], F32, name="bias")
-        pages = [keep.tile([P, T], F32, name="page%d" % m) for m in range(2)]
+        bias = keep.tile([P, PAGES, BIAS_PITCH], F32, name="bias")
+        pages = [keep.tile([P, T], F32, name="page%d" % m) for m in range(PAGES)]
         warm_in = keep.tile([P, 1], F32, name="warm_in")
         warm_out = keep.tile([P, 1], F32, name="warm_out")
 
@@ -54,104 +76,118 @@ def tile_list_tabhs_d_gelu_kernel(tc, tab, w4_words, w4_scales, c, u, b, wgo, of
         nc.vector.memset(warm_in[:], 0.0)
         nc.vector.memset(w4_plane[:].bitcast(I32), 0)
         nc.scalar.activation(warm_out[:], warm_in[:], GELU)
-        for m in range(2):
+        for m in range(PAGES):
             nc.vector.memset(pages[m][:], 0.0)
 
-        c_rows = c.rearrange("(p t) j -> p t j", t=PACK)
-        tab_scales = tab[0, K * T :].rearrange("(q t) -> q t", t=T)
-
-        def load_scale_rows(queue, plane, rows, q):
-            queue.dma_start(plane[32 * q : 32 * q + 4, :].bitcast(I32), rows[4 * q : 4 * q + 4, :].bitcast(I32))
-
         nc.gpsimd.dma_start(w4_codes[:].bitcast(I32), w4_words[0].bitcast(I32))
-        with nc.allow_non_contiguous_dma(reason="one bias value a partition"):
+        with nc.allow_non_contiguous_dma(reason="one bias value a partition and page"):
             nc.gpsimd.dma_start(bias[:, :, 0], b.rearrange("(m p) -> p m", p=P))
 
+        c_rows = c.rearrange("(p t) j -> p t j", t=PACK)
         nc.sync.dma_start(u_raw[:], u.rearrange("(p t) n -> p t n", t=PACK))
         nc.sync.dma_start(pick[:], offs)
-        for q in range(4):
-            load_scale_rows(nc.sync, tab_plane, tab_scales, q)
+        load_scale_rows(nc, tab_plane, tab[0, K * T :].rearrange("(q x) -> q x", x=T))
         nc.sync.dma_start(c_raw[0][:], c_rows[:, :, 0:HALF])
         nc.sync.dma_start(tab_words[:], tab[0, 0 : K * T].rearrange("(p x) -> p x", p=P).bitcast(I32))
-        for q in range(4):
-            load_scale_rows(nc.sync, w4_plane, w4_scales[0], q)
+        load_scale_rows(nc, w4_plane, w4_scales[0])
         nc.sync.dma_start(place[:], offs2)
         nc.sync.dma_start(weight[0][:], wgo[:, 0:HALF])
         nc.sync.dma_start(c_raw[1][:], c_rows[:, :, HALF:S])
         nc.sync.dma_start(weight[1][:], wgo[:, HALF:S])
 
-        picked_plane = keep.tile([P, S], U8, name="picked_plane", align_bytes=64)
+        picked_plane = keep.tile([P, S], U8, name="picked_plane", align_bytes=MX_ALIGN)
         nc.vector.tensor_copy(picked_plane[:], tab_plane[:].indirect(pick[:]))
 
-        u_grouped = keep.tile([P, M, PACK], BF16, name="u_grouped", align_bytes=64)
-        u_codes = keep.tile([P, M], U32, name="u_codes", tag="tab_plane", align_bytes=64)
-        u_plane = keep.tile([P, M], U8, name="u_plane", align_bytes=64)
-        interleave(nc.scalar.copy, u_grouped[:], u_raw[:])
-        nc.vector.quantize_mx(u_codes[:].bitcast(FP8X4), u_plane[:], u_grouped[:].rearrange("p n t -> p (n t)"))
+        u_grouped = keep.tile([P, M, PACK], BF16, name="u_grouped", align_bytes=MX_ALIGN)
+        u_codes = keep.tile([P, M], U32, name="u_codes", tag="tab_plane", align_bytes=MX_ALIGN)
+        u_plane = keep.tile([P, M], U8, name="u_plane", align_bytes=MX_ALIGN)
+        round_and_interleave(nc, u_grouped[:], u_raw[:])
+        quantise(nc, u_codes, u_plane, u_grouped)
 
         c_codes = []
         c_plane = []
-        picked_words = []
+        picked_words = keep.tile([P, S], U32, name="picked_words", align_bytes=MX_ALIGN)
 
-        def quantise_c(i, copy):
-            j0, width = CHUNKS[i]
-            grouped = keep.tile([P, width, PACK], BF16, name="c_grouped%d" % i, align_bytes=64)
-            codes = keep.tile([P, width], U32, name="c_codes%d" % i, align_bytes=64)
-            plane = keep.tile([P, width], U8, name="c_plane%d" % i, align_bytes=64)
-            interleave(copy, grouped[:], c_raw[j0 // HALF][:, :, j0 % HALF : j0 % HALF + width])
-            nc.vector.quantize_mx(codes[:].bitcast(FP8X4), plane[:], grouped[:].rearrange("p n t -> p (n t)"))
+        def in_half(chunk):
+            first, count = CHUNKS[chunk]
+            return first // HALF, slice(first % HALF, first % HALF + count)
+
+        def quantise_c(chunk):
+            count = CHUNKS[chunk][1]
+            half, cols = in_half(chunk)
+            grouped = keep.tile([P, count, PACK], BF16, name="c_grouped%d" % chunk, align_bytes=MX_ALIGN)
+            codes = keep.tile([P, count], U32, name="c_codes%d" % chunk, align_bytes=MX_ALIGN)
+            plane = keep.tile([P, count], U8, name="c_plane%d" % chunk, align_bytes=MX_ALIGN)
+            round_and_interleave(nc, grouped[:], c_raw[half][:, :, cols])
+            quantise(nc, codes, plane, grouped)
             c_codes.append(codes)
             c_plane.append(plane)
 
-        def gather_words(i):
-            j0, width = CHUNKS[i]
-            words = keep.tile([P, width], U32, name="picked_words%d" % i, align_bytes=64)
-            nc.vector.tensor_copy(words[:], tab_words[:].bitcast(U32).indirect(pick[:, j0 // LANES : (j0 + width) // LANES]))
-            picked_words.append(words)
+        def gather_words(first, count):
+            window = tab_words[:].bitcast(U32)
+            nc.vector.tensor_copy(
+                picked_words[:, first : first + count], window.indirect(pick[:, list_columns(first, count)])
+            )
 
-        def project(i, m, act):
-            j0, width = CHUNKS[i]
-            acc = psum.tile([P, width], F32, name="acc%d_%d" % (i, m))
+        def project(chunk, m, act):
+            first, count = CHUNKS[chunk]
+            half, cols = in_half(chunk)
+            acc = psum.tile([P, count], F32, name="acc%d_%d" % (chunk, m))
             rows = slice(m * P, (m + 1) * P)
-            pieces = width // P
+            pieces = count // FP4_N
 
-            def dense(start, stop):
-                nc.tensor.matmul_mx(acc[:], lhsT=u_codes[:, rows].bitcast(FP8X4), lhsT_scale=u_plane[:, rows],
-                                    rhs=c_codes[i][:].bitcast(FP8X4), rhs_scale=c_plane[i][:], start=start, stop=stop)
+            def dense_pass(start, stop):
+                nc.tensor.matmul_mx(
+                    acc[:],
+                    lhsT=u_codes[:, rows].bitcast(FP8X4),
+                    lhsT_scale=u_plane[:, rows],
+                    rhs=c_codes[chunk][:].bitcast(FP8X4),
+                    rhs_scale=c_plane[chunk][:],
+                    start=start,
+                    stop=stop,
+                )
 
-            def looked_up(n, start, stop):
-                cols = slice(n * P, (n + 1) * P)
-                nc.tensor.matmul_mx(acc[:, cols], lhsT=w4_codes[:, 2 * m * P : 2 * (m + 1) * P].bitcast(FP4X4), lhsT_scale=w4_plane[:, rows],
-                                    rhs=picked_words[i][:, cols].bitcast(FP8X4), rhs_scale=picked_plane[:, j0 + n * P : j0 + (n + 1) * P],
-                                    start=start, stop=stop)
+            def table_pass(piece, start, stop):
+                picked = slice(first + piece * FP4_N, first + (piece + 1) * FP4_N)
+                nc.tensor.matmul_mx(
+                    acc[:, piece * FP4_N : (piece + 1) * FP4_N],
+                    lhsT=w4_codes[:, 2 * m * P : 2 * (m + 1) * P].bitcast(FP4X4),
+                    lhsT_scale=w4_plane[:, rows],
+                    rhs=picked_words[:, picked].bitcast(FP8X4),
+                    rhs_scale=picked_plane[:, picked],
+                    start=start,
+                    stop=stop,
+                )
 
-            if j0 < HALF:
-                dense(True, False)
-                for n in range(pieces):
-                    looked_up(n, False, n == pieces - 1)
+            if chunk == 0:
+                dense_pass(True, False)
+                for piece in range(pieces):
+                    table_pass(piece, False, piece == pieces - 1)
             else:
-                for n in range(pieces):
-                    looked_up(n, n == 0, False)
-                dense(False, True)
+                for piece in range(pieces):
+                    table_pass(piece, piece == 0, False)
+                dense_pass(False, True)
 
             nc.scalar.activation(act, acc[:], GELU, bias=bias[:, m, 0:1])
-            nc.vector.tensor_tensor(pages[m][:].indirect(place[:, j0 // LANES : (j0 + width) // LANES]), act,
-                                    weight[j0 // HALF][:, j0 % HALF : j0 % HALF + width], MULT)
+            nc.vector.tensor_tensor(
+                pages[m][:].indirect(place[:, list_columns(first, count)]), act, weight[half][:, cols], MULT
+            )
 
-        quantise_c(0, nc.scalar.copy)
-        gather_words(0)
-        quantise_c(1, nc.scalar.copy)
-        gather_words(1)
-        gather_words(2)
-        act0 = keep.tile([P, 2, 128], F32, name="act0")
-        for m in range(2):
-            project(0, m, act0[:, m, :])
-        quantise_c(2, nc.scalar.copy)
-        act1 = keep.tile([P, 2, 128], F32, name="act1", tag="c_raw1")
-        for m in range(2):
-            project(1, m, act1[:, m, :])
-        act2 = keep.tile([P, 2, 256], F32, name="act2")
-        for m in range(2):
-            project(2, m, act2[:, m, :])
-        for m in range(2):
+        def project_pages(chunk, tag):
+            act = keep.tile([P, PAGES, CHUNKS[chunk][1]], F32, name="act%d" % chunk, tag=tag)
+            for m in range(PAGES):
+                project(chunk, m, act[:, m, :])
+
+        first_count = CHUNKS[0][1]
+        quantise_c(0)
+        gather_words(0, first_count)
+        quantise_c(1)
+        gather_words(first_count, S - first_count)
+
+        project_pages(0, "act0")
+        quantise_c(2)
+        project_pages(1, "c_raw1")
+        project_pages(2, "act2")
+
+        for m in range(PAGES):
             nc.sync.dma_start(out[m * P : (m + 1) * P, :], pages[m][:])

from contextlib import ExitStack

import concourse.mybir as mybir

K, M, T, S = 512, 256, 1024, 512
FLOPS = 2 * 2 * K * M * S

F32 = mybir.dt.float32
BF16 = mybir.dt.bfloat16
I32 = mybir.dt.int32
U32 = mybir.dt.uint32
U16 = mybir.dt.uint16
U8 = mybir.dt.uint8
FP8X4 = mybir.dt.float8_e4m3fn_x4
FP4X4 = mybir.dt.float4_e2m1fn_x4
GELU = mybir.ActivationFunctionType.Gelu_apprx_tanh
MULT = mybir.AluOpType.mult

P = 128
PACK = 4
QUADRANT = 32
GROUP = 16
PAGES = M // P
HALF = S // 2
FP4_N = 128
BIAS_PITCH = 8
MX_ALIGN = 64

CHUNKS = ((0, 128), (128, 128), (256, 256))


def round_and_interleave(nc, grouped, raw):
    nc.scalar.copy(
        grouped.rearrange("p (c i) t -> p c t i", i=PACK),
        raw.rearrange("p t (c i) -> p c t i", i=PACK),
    )


def quantise(nc, codes, plane, grouped):
    nc.vector.quantize_mx(codes[:].bitcast(FP8X4), plane[:], grouped[:].rearrange("p x t -> p (x t)"))


def load_scale_rows(nc, plane, rows):
    for quad in range(P // QUADRANT):
        nc.sync.dma_start(
            plane[QUADRANT * quad : QUADRANT * quad + PACK, :].bitcast(I32),
            rows[PACK * quad : PACK * (quad + 1), :].bitcast(I32),
        )


def list_columns(first, count):
    return slice(first // GROUP, (first + count) // GROUP)


def tile_list_tabhs_d_gelu_kernel(tc, tab, w4_words, w4_scales, c, u, b, wgo, offs, offs2, out):
    nc = tc.nc
    with ExitStack() as ctx:
        keep = ctx.enter_context(tc.tile_pool(name="keep", bufs=1))
        psum = ctx.enter_context(tc.psum_pool(name="psum", bufs=1))

        pick = keep.tile([P, S // GROUP], U16, name="pick")
        place = keep.tile([P, S // GROUP], U16, name="place")
        tab_words = keep.tile([P, T], I32, name="tab_words", align_bytes=MX_ALIGN)
        tab_plane = keep.tile([P, T], U8, name="tab_plane", tag="tab_plane", align_bytes=MX_ALIGN)
        w4_codes = keep.tile([P, 2 * M], U8, name="w4_codes", align_bytes=MX_ALIGN)
        w4_plane = keep.tile([P, M], U8, name="w4_plane", align_bytes=MX_ALIGN)
        u_raw = keep.tile([P, PACK, M], F32, name="u_raw")
        c_raw = [keep.tile([P, PACK, HALF], F32, name="c_raw%d" % h, tag="c_raw%d" % h) for h in range(2)]
        weight = [keep.tile([P, HALF], F32, name="weight%d" % h) for h in range(2)]
        bias = keep.tile([P, PAGES, BIAS_PITCH], F32, name="bias")
        pages = [keep.tile([P, T], F32, name="page%d" % m) for m in range(PAGES)]
        warm_in = keep.tile([P, 1], F32, name="warm_in")
        warm_out = keep.tile([P, 1], F32, name="warm_out")

        nc.vector.memset(tab_plane[:].bitcast(I32), 0)
        nc.vector.memset(warm_in[:], 0.0)
        nc.vector.memset(w4_plane[:].bitcast(I32), 0)
        nc.scalar.activation(warm_out[:], warm_in[:], GELU)
        for m in range(PAGES):
            nc.vector.memset(pages[m][:], 0.0)

        nc.gpsimd.dma_start(w4_codes[:].bitcast(I32), w4_words[0].bitcast(I32))
        with nc.allow_non_contiguous_dma(reason="one bias value a partition and page"):
            nc.gpsimd.dma_start(bias[:, :, 0], b.rearrange("(m p) -> p m", p=P))

        c_rows = c.rearrange("(p t) j -> p t j", t=PACK)
        nc.sync.dma_start(u_raw[:], u.rearrange("(p t) n -> p t n", t=PACK))
        nc.sync.dma_start(pick[:], offs)
        load_scale_rows(nc, tab_plane, tab[0, K * T :].rearrange("(q x) -> q x", x=T))
        nc.sync.dma_start(c_raw[0][:], c_rows[:, :, 0:HALF])
        nc.sync.dma_start(tab_words[:], tab[0, 0 : K * T].rearrange("(p x) -> p x", p=P).bitcast(I32))
        load_scale_rows(nc, w4_plane, w4_scales[0])
        nc.sync.dma_start(place[:], offs2)
        nc.sync.dma_start(weight[0][:], wgo[:, 0:HALF])
        nc.sync.dma_start(c_raw[1][:], c_rows[:, :, HALF:S])
        nc.sync.dma_start(weight[1][:], wgo[:, HALF:S])

        picked_plane = keep.tile([P, S], U8, name="picked_plane", align_bytes=MX_ALIGN)
        nc.vector.tensor_copy(picked_plane[:], tab_plane[:].indirect(pick[:]))

        u_grouped = keep.tile([P, M, PACK], BF16, name="u_grouped", align_bytes=MX_ALIGN)
        u_codes = keep.tile([P, M], U32, name="u_codes", tag="tab_plane", align_bytes=MX_ALIGN)
        u_plane = keep.tile([P, M], U8, name="u_plane", align_bytes=MX_ALIGN)
        round_and_interleave(nc, u_grouped[:], u_raw[:])
        quantise(nc, u_codes, u_plane, u_grouped)

        c_codes = []
        c_plane = []
        picked_words = keep.tile([P, S], U32, name="picked_words", align_bytes=MX_ALIGN)

        def in_half(chunk):
            first, count = CHUNKS[chunk]
            return first // HALF, slice(first % HALF, first % HALF + count)

        def quantise_c(chunk):
            count = CHUNKS[chunk][1]
            half, cols = in_half(chunk)
            grouped = keep.tile([P, count, PACK], BF16, name="c_grouped%d" % chunk, align_bytes=MX_ALIGN)
            codes = keep.tile([P, count], U32, name="c_codes%d" % chunk, align_bytes=MX_ALIGN)
            plane = keep.tile([P, count], U8, name="c_plane%d" % chunk, align_bytes=MX_ALIGN)
            round_and_interleave(nc, grouped[:], c_raw[half][:, :, cols])
            quantise(nc, codes, plane, grouped)
            c_codes.append(codes)
            c_plane.append(plane)

        def gather_words(first, count):
            window = tab_words[:].bitcast(U32)
            nc.vector.tensor_copy(
                picked_words[:, first : first + count], window.indirect(pick[:, list_columns(first, count)])
            )

        def project(chunk, m, act):
            first, count = CHUNKS[chunk]
            half, cols = in_half(chunk)
            acc = psum.tile([P, count], F32, name="acc%d_%d" % (chunk, m))
            rows = slice(m * P, (m + 1) * P)
            pieces = count // FP4_N

            def dense_pass(start, stop):
                nc.tensor.matmul_mx(
                    acc[:],
                    lhsT=u_codes[:, rows].bitcast(FP8X4),
                    lhsT_scale=u_plane[:, rows],
                    rhs=c_codes[chunk][:].bitcast(FP8X4),
                    rhs_scale=c_plane[chunk][:],
                    start=start,
                    stop=stop,
                )

            def table_pass(piece, start, stop):
                picked = slice(first + piece * FP4_N, first + (piece + 1) * FP4_N)
                nc.tensor.matmul_mx(
                    acc[:, piece * FP4_N : (piece + 1) * FP4_N],
                    lhsT=w4_codes[:, 2 * m * P : 2 * (m + 1) * P].bitcast(FP4X4),
                    lhsT_scale=w4_plane[:, rows],
                    rhs=picked_words[:, picked].bitcast(FP8X4),
                    rhs_scale=picked_plane[:, picked],
                    start=start,
                    stop=stop,
                )

            if chunk == 0:
                dense_pass(True, False)
                for piece in range(pieces):
                    table_pass(piece, False, piece == pieces - 1)
            else:
                for piece in range(pieces):
                    table_pass(piece, piece == 0, False)
                dense_pass(False, True)

            nc.scalar.activation(act, acc[:], GELU, bias=bias[:, m, 0:1])
            nc.vector.tensor_tensor(
                pages[m][:].indirect(place[:, list_columns(first, count)]), act, weight[half][:, cols], MULT
            )

        def project_pages(chunk, tag):
            act = keep.tile([P, PAGES, CHUNKS[chunk][1]], F32, name="act%d" % chunk, tag=tag)
            for m in range(PAGES):
                project(chunk, m, act[:, m, :])

        first_count = CHUNKS[0][1]
        quantise_c(0)
        gather_words(0, first_count)
        quantise_c(1)
        gather_words(first_count, S - first_count)

        project_pages(0, "act0")
        quantise_c(2)
        project_pages(1, "c_raw1")
        project_pages(2, "act2")

        for m in range(PAGES):
            nc.sync.dma_start(out[m * P : (m + 1) * P, :], pages[m][:])
